import numpy as np
import ml_dtypes


def mxq(x, axis, fmt="e4m3"):
    dtype, down = {"e4m3": (ml_dtypes.float8_e4m3fn, 7), "e5m2": (ml_dtypes.float8_e5m2, 14)}[fmt]
    v = np.moveaxis(np.asarray(x, np.float32).astype(ml_dtypes.bfloat16).astype(np.float64), axis, -1)
    blocks = v.reshape(v.shape[:-1] + (-1, 32))
    amax = np.abs(blocks).max(-1, keepdims=True)
    byte = np.maximum(np.where(amax > 0, np.frexp(amax)[1] - 1 + 127, 0) - down, 1)
    scale = np.exp2(byte - 127.0)
    codes = (blocks / scale).astype(np.float32).astype(dtype).astype(np.float64)
    return np.moveaxis((codes * scale).reshape(v.shape), -1, axis)


WIDE = False


def mx_kscale(k):
    if not WIDE:
        return np.ones(k)
    levels = np.array([10, -10, 5, -5, 0])
    if k % 512:
        return np.exp2(np.random.permutation(np.resize(levels, k // 32))).repeat(32)
    a = np.empty((k // 512, 16))
    for p in range(k // 512):
        a[p, :8] = np.random.permutation(np.resize(levels, 8))
        for g in range(8):
            far = levels[np.abs(levels - a[p, g]) >= 10]
            a[p, g + 8] = far[np.random.randint(len(far))]
    return np.exp2(a.ravel()).repeat(32)


def f64(x):
    return np.asarray(x).astype(np.float64)


def striped(idx):
    return np.tile(idx.reshape(-1, 16).T, (8, 1)).astype(np.uint16)


def unstriped(offs):
    return offs[:16].T.reshape(-1).astype(np.int64)


def pack_weight(w):
    k, n = w.shape
    w = f64(np.asarray(w, np.float32).astype(ml_dtypes.bfloat16)).reshape(k // 32, 32, n)
    amax = np.abs(w).max(1)
    byte = np.clip(np.where(amax > 0, np.frexp(amax)[1] - 1 + 127 - 7, 1), 1, 254)
    scaled = (w * np.exp2(127.0 - byte)[:, None, :]).reshape(k, n).astype(np.float32)
    words = np.ascontiguousarray(scaled.reshape(k // 512, 128, 4, n).transpose(0, 1, 3, 2)).astype(ml_dtypes.float8_e4m3fn).view(np.uint8)
    return words, np.ascontiguousarray(byte.astype(np.uint8).reshape(k // 512, 16, n))


def unpack_weight(words, scales):
    g, p, n, _ = words.shape
    vals = np.ascontiguousarray(words).view(ml_dtypes.float8_e4m3fn).astype(np.float64) * np.repeat(np.exp2(scales.astype(np.float64) - 127.0), 8, axis=1)[..., None]
    return vals.transpose(0, 1, 3, 2).reshape(g * 512, n)


E2M1 = np.array([0.0, 0.5, 1.0, 1.5, 2.0, 3.0, 4.0, 6.0, -0.0, -0.5, -1.0, -1.5, -2.0, -3.0, -4.0, -6.0])


def pack_fp4(w):
    k, n = w.shape
    w = f64(np.asarray(w, np.float32).astype(ml_dtypes.bfloat16)).reshape(k // 32, 32, n)
    amax = np.abs(w).max(1)
    mant, ex = np.frexp(amax / 6.0)
    byte = np.clip(np.where(amax > 0, np.where(mant > 0.5, ex, ex - 1) + 127, 1), 1, 254)
    scaled = (w * np.exp2(127.0 - byte)[:, None, :]).reshape(k, n).astype(np.float32)
    c = np.ascontiguousarray(scaled.reshape(k // 512, 128, 4, n).transpose(0, 1, 3, 2)).astype(ml_dtypes.float4_e2m1fn).view(np.uint8) & 0xF
    words = (c[..., 0::2] | (c[..., 1::2] << 4)).reshape(k // 512, 128, 2 * n)
    return np.ascontiguousarray(words), np.ascontiguousarray(byte.astype(np.uint8).reshape(k // 512, 16, n))


def unpack_fp4(words, scales):
    g, _, n = scales.shape
    words = np.ascontiguousarray(words).reshape(g, 128, n, 2)
    nib = np.empty((g, 128, n, 4), np.uint8)
    nib[..., 0::2] = words & 0xF
    nib[..., 1::2] = words >> 4
    vals = E2M1[nib] * np.repeat(np.exp2(scales.astype(np.float64) - 127.0), 8, axis=1)[..., None]
    return vals.transpose(0, 1, 3, 2).reshape(g * 512, n)


def planes(y):
    n, m = y.shape
    v = y.astype(np.float32).astype(ml_dtypes.bfloat16).astype(np.float64).reshape(n // 32, 32, m)
    top = np.abs(v).max(1)
    byte = np.clip(np.where(top > 0, np.frexp(top)[1] - 1 + 127 - 7, 1), 1, 254)
    codes = (v * np.exp2(127.0 - byte)[:, None, :]).reshape(n, m).astype(np.float32).astype(ml_dtypes.float8_e4m3fn).view(np.uint8)
    words = codes.reshape(n // 512, 128, 4, m).transpose(0, 1, 3, 2)
    return np.ascontiguousarray(words), np.ascontiguousarray(byte.astype(np.uint8).reshape(n // 512, 16, m))


def gelu(v):
    return 0.5 * v * (1.0 + np.tanh(np.sqrt(2.0 / np.pi) * (v + 0.044715 * v**3)))


K, T, S, H, Z, W = 512, 2048, 512, 512, 512, 1024
P = 2 ** 7


def setup_inputs():
    n = np.random.standard_normal
    s = mx_kscale(K)[:, None]
    u = mx_kscale(H)
    packed_xT = pack_weight(n((K, T)) * s)
    packed_w1 = pack_fp4(n((K, H)) / np.sqrt(K) / s)
    packed_w2 = pack_fp4(n((K, H)) / np.sqrt(K) / s)
    packed_eT = pack_weight(n((K, W)) * s)
    packed_w3 = pack_fp4(n((K, H)) / np.sqrt(K) / s)
    return {
        "x_words": packed_xT[0],
        "x_scales": packed_xT[1],
        "w1_words": packed_w1[0],
        "w1_scales": packed_w1[1],
        "w2_words": packed_w2[0],
        "w2_scales": packed_w2[1],
        "e_words": packed_eT[0],
        "e_scales": packed_eT[1],
        "w3_words": packed_w3[0],
        "w3_scales": packed_w3[1],
        "unit": (np.random.uniform(0.6, 1.4, (H, 1)) * u[:, None]).astype(np.float32),
        "unit2": (np.random.uniform(0.6, 1.4, (H, 1)) / np.sqrt(H) / u[:, None]).astype(np.float32),
        "rad": (np.tile(np.random.uniform(0.2, 1.0, W), (P, 1))).astype(np.float32),
        "offs": striped(np.random.permutation(T)[:S]),
        "obs_": striped(np.random.permutation(W)[:Z]),
        "par": striped(np.random.permutation(S)),
        "nxo": striped(np.random.permutation(Z)),
    }


def reference(x_words, x_scales, w1_words, w1_scales, w2_words, w2_scales, e_words, e_scales, w3_words, w3_scales, unit, unit2, rad, offs, obs_, par, nxo):
    xq = unpack_weight(x_words, x_scales)[:, unstriped(offs)]
    y = unpack_fp4(w1_words, w1_scales).T @ xq
    yv = unpack_fp4(w2_words, w2_scales).T @ xq
    vp = yv[:, unstriped(par)]
    pos = y + 0.6 * vp
    hid = f64(unit) * pos
    e_obs_ = unpack_weight(e_words, e_scales)[:, unstriped(obs_)]
    ye = unpack_fp4(w3_words, w3_scales).T @ e_obs_
    obst = gelu(ye)
    hid2 = f64(unit2) * obst
    sc = mxq(hid, 0, "e4m3").T @ mxq(hid2, 0, "e4m3")
    clr = np.abs(sc) + 0.1 - (f64(rad)[:1][:, unstriped(obs_)])
    pen = np.log(np.exp(-2.0 * clr) + 1.0)
    dn_ = clr[:, unstriped(nxo)]
    out_0 = pen * sc - (0.3 * dn_)
    return (out_0,) + planes(out_0)

@@ -1,0 +1,296 @@
+from contextlib import ExitStack
+
+import concourse.mybir as mybir
+from concourse.masks import make_identity
+
+F32 = mybir.dt.float32
+BF16 = mybir.dt.bfloat16
+I32 = mybir.dt.int32
+U32 = mybir.dt.uint32
+U16 = mybir.dt.uint16
+U8 = mybir.dt.uint8
+FP8X4 = mybir.dt.float8_e4m3fn_x4
+FP4X4 = mybir.dt.float4_e2m1fn_x4
+ALU = mybir.AluOpType
+ACT = mybir.ActivationFunctionType
+
+P = 128
+PACK = 4
+N = 512
+T_LINKS = 2048
+T_OBST = 1024
+HALF = N // 2
+QUARTER = N // 4
+PAD = 16
+FUSED = 3
+CLR_FLOOR = -15.0
+
+FLOPS = 4 * 2 * N * N * N
+
+
+def tile_picked_ycollid_way_po_kernel(
+    tc, x_words, x_scales, w1_words, w1_scales, w2_words, w2_scales, e_words, e_scales,
+    w3_words, w3_scales, unit, unit2, rad, offs, obs_, par, nxo, out_0, out_1, out_2,
+):
+    nc = tc.nc
+    with ExitStack() as ctx:
+        sb = ctx.enter_context(tc.tile_pool(name="sb", bufs=1))
+        psum = ctx.enter_context(tc.psum_pool(name="psum", bufs=1))
+
+        def sbuf(name, shape, dtype, tag=None):
+            return sb.tile(shape, dtype, name=name, tag=tag or name, align_bytes=64)
+
+        def bank(name, shape, tag):
+            return psum.tile(shape, F32, name=name, tag=tag)
+
+        def load_list(name, src):
+            t = sbuf(name, [P, N // 16], U16)
+            nc.sync.dma_start(t[:], src)
+            return t
+
+        def load_scale_rows(queue, dst, src):
+            for q in range(4):
+                queue.dma_start(out=dst[32 * q : 32 * q + 4, :].bitcast(I32), in_=src[0, 4 * q : 4 * q + 4, :].bitcast(I32))
+
+        def load_words(dst, src):
+            nc.sync.dma_start(out=dst[:].bitcast(I32), in_=src[0].rearrange("p n r -> p (n r)").bitcast(I32))
+
+        e_sc_tab = sbuf("e_sc_tab", [P, T_OBST], U8)
+        x_sc_tab = sbuf("x_sc_tab", [P, T_LINKS], U8)
+        w3_sc_raw = sbuf("w3_sc_raw", [P, N], U8)
+        w21_sc_raw = sbuf("w21_sc_raw", [P, 2 * N], U8)
+        unit_rows = sbuf("unit_rows", [P, P], F32)
+        nc.gpsimd.memset(w3_sc_raw[:].bitcast(I32), 0)
+        for t in (e_sc_tab, x_sc_tab, w21_sc_raw):
+            nc.vector.memset(t[:].bitcast(I32), 0)
+        nc.vector.memset(unit_rows[:], 0.0)
+
+        load_scale_rows(nc.gpsimd, w3_sc_raw, w3_scales)
+        for i, src in enumerate((unit2, unit)):
+            nc.gpsimd.dma_start(
+                out=unit_rows[4 * i : 4 * i + 4, :].rearrange("t (b r) -> t b r", r=8),
+                in_=src.rearrange("(b t r) o -> t b (r o)", t=4, r=8),
+            )
+
+        w3_raw = sbuf("w3_raw", [P, 1, 2 * N // 4], I32)
+        w21_raw = sbuf("w21_raw", [P, 2, 2 * N // 4], I32)
+        obs_t = load_list("obs_t", obs_)
+        e_tab = sbuf("e_tab", [P, T_OBST], U32)
+        load_words(e_tab, e_words)
+        nc.sync.dma_start(out=w3_raw[:, 0, :], in_=w3_words[0].bitcast(I32))
+        load_scale_rows(nc.sync, e_sc_tab, e_scales)
+        offs_t = load_list("offs_t", offs)
+        x_tab = sbuf("x_tab", [P, T_LINKS], U32)
+        load_words(x_tab, x_words)
+        load_scale_rows(nc.sync, x_sc_tab, x_scales)
+        nc.sync.dma_start(out=w21_raw[:, 0, :], in_=w2_words[0].bitcast(I32))
+        nc.sync.dma_start(out=w21_raw[:, 1, :], in_=w1_words[0].bitcast(I32))
+        par_t = load_list("par_t", par)
+        load_scale_rows(nc.sync, w21_sc_raw[:, 0:N], w2_scales)
+        load_scale_rows(nc.sync, w21_sc_raw[:, N : 2 * N], w1_scales)
+        nxo_t = load_list("nxo_t", nxo)
+
+        def deal_weights(engine, name, count, raw, sc_raw):
+            words = sbuf(name, [P, count * 2 * N], U8)
+            scales = sbuf(name + "_sc", [P, count * N], U8)
+            engine.tensor_copy(
+                out=words[:].bitcast(I32).rearrange("p (w t b r) -> p w t b r", w=count, t=4, r=4),
+                in_=raw[:].rearrange("p w (b t r) -> p w t b r", t=4, r=4),
+            )
+            engine.tensor_copy(
+                out=scales[:].bitcast(I32).rearrange("p (w t b r) -> p w t b r", w=count, t=4, r=2),
+                in_=sc_raw[:].bitcast(I32).rearrange("p (w b t r) -> p w t b r", w=count, t=4, r=2),
+            )
+            return words, scales
+
+        e_codes = sbuf("e_codes", [P, N], U32)
+        e_sc = sbuf("e_sc", [P, N], U8)
+        nc.vector.tensor_copy(out=e_codes[:], in_=e_tab[:].indirect(obs_t[:]))
+        nc.vector.tensor_copy(out=e_sc[:], in_=e_sc_tab[:].indirect(obs_t[:]))
+        w3, w3_sc = deal_weights(nc.gpsimd, "w3", 1, w3_raw, w3_sc_raw)
+        rad_tab = sbuf("rad_tab", [P, T_OBST], F32, tag="e_tab")
+        nc.sync.dma_start(out=rad_tab[:], in_=rad)
+        x_codes = sbuf("x_codes", [P, N], U32)
+        x_sc = sbuf("x_sc", [P, N], U8)
+        nc.vector.tensor_copy(out=x_codes[:], in_=x_tab[:].indirect(offs_t[:]))
+        nc.vector.tensor_copy(out=x_sc[:], in_=x_sc_tab[:].indirect(offs_t[:]))
+        w21, w21_sc = deal_weights(nc.vector, "w21", 2, w21_raw, w21_sc_raw)
+
+        ident = sbuf("ident", [P, P], F32, tag="w3_sc_raw")
+        make_identity(nc, ident[:])
+        unit_ps = bank("unit_ps", [P, P], "b3")
+        nc.tensor.transpose(unit_ps[:], unit_rows[:], ident[:])
+        units = sbuf("units", [P, 8], F32, tag="x_tab")
+        unit06 = sbuf("unit06", [P, 4], F32)
+        nc.vector.tensor_copy(out=units[:], in_=unit_ps[:, 0:8])
+        nc.gpsimd.tensor_scalar(out=unit06[:], in0=units[:, 4:8], scalar1=0.6, scalar2=None, op0=ALU.mult)
+
+        def weight_product(out, words, scales, col0, codes, code_scales):
+            nc.tensor.matmul_mx(
+                out=out,
+                lhsT=words[:, 2 * col0 : 2 * (col0 + P)].bitcast(FP4X4),
+                lhsT_scale=scales[:, col0 : col0 + P],
+                rhs=codes.bitcast(FP8X4),
+                rhs_scale=code_scales,
+                start=True,
+                stop=True,
+            )
+
+        hid2_bf = sbuf("hid2_bf", [P, N * PACK], BF16, tag="w21_sc_raw")
+        for q in range(4):
+            cols = slice(q * QUARTER, (q + 1) * QUARTER)
+            ye = bank("ye%d" % q, [P, PACK, QUARTER], "a%d" % q)
+            for t in range(PACK):
+                weight_product(ye[:, t, :], w3, w3_sc, t * P, e_codes[:, cols], e_sc[:, cols])
+            obst = sbuf("obst%d" % q, [P, QUARTER, PACK], F32)
+            nc.scalar.activation(out=obst[:], in_=ye[:].rearrange("p t n -> p n t"), func=ACT.Gelu_apprx_tanh)
+            nc.vector.tensor_tensor(
+                out=hid2_bf[:, q * N : (q + 1) * N].rearrange("p (n t) -> p n t", t=PACK),
+                in0=obst[:],
+                in1=units[:, 0:4].unsqueeze(1).to_broadcast([P, QUARTER, PACK]),
+                op=ALU.mult,
+            )
+        hid2_codes = sbuf("hid2_codes", [P, N], U32)
+        hid2_sc = sbuf("hid2_sc", [P, N], U8)
+        nc.vector.quantize_mx(out=hid2_codes[:].bitcast(FP8X4), scales=hid2_sc[:], in_=hid2_bf[:])
+
+        hid = sbuf("hid", [P, PACK, N], F32)
+        for t in range(PACK):
+            yv = bank("yv%d" % t, [P, N], "b%d" % t)
+            weight_product(yv[:], w21, w21_sc, t * P, x_codes[:], x_sc[:])
+            y = bank("y%d" % t, [P, N], "a%d" % t)
+            weight_product(y[:], w21, w21_sc, N + t * P, x_codes[:], x_sc[:])
+            yv_s = sbuf("yv_s%d" % t, [P, N + PAD], F32)
+            nc.vector.memset(yv_s[:, N:], 0.0)
+            nc.scalar.activation(out=yv_s[:, :N], in_=yv[:], func=ACT.Copy, scale=unit06[:, t : t + 1])
+            part = sbuf("part%d" % t, [P, N], F32)
+            if t < FUSED:
+                nc.scalar.activation(out=part[:], in_=y[:], func=ACT.Copy, scale=units[:, 4 + t : 5 + t])
+                nc.vector.tensor_tensor(out=hid[:, t, :], in0=yv_s[:].indirect(par_t[:]), in1=part[:], op=ALU.add)
+            else:
+                nc.scalar.activation(out=part[:], in_=yv_s[:].indirect(par_t[:]), func=ACT.Copy)
+                nc.vector.scalar_tensor_tensor(
+                    out=hid[:, t, :], in0=y[:], scalar=units[:, 4 + t : 5 + t], in1=part[:], op0=ALU.mult, op1=ALU.add
+                )
+        radg = sbuf("radg", [P, N], F32, tag="yv_s3")
+        nc.scalar.activation(out=radg[:], in_=rad_tab[:].indirect(obs_t[:]), func=ACT.Copy)
+
+        hid_bf = sbuf("hid_bf", [P, N * PACK], BF16)
+        nc.vector.tensor_copy(
+            out=hid_bf[:].rearrange("p (j m t) -> p m t j", j=PACK, t=PACK),
+            in_=hid[:].rearrange("p t (m j) -> p m t j", j=PACK),
+        )
+        hid_codes = sbuf("hid_codes", [P, N], U32)
+        hid_sc = sbuf("hid_sc", [P, N], U8)
+        nc.vector.quantize_mx(out=hid_codes[:].bitcast(FP8X4), scales=hid_sc[:], in_=hid_bf[:])
+
+        clr = sbuf("clr", [P, PACK, N], F32)
+        expo = sbuf("expo", [P, 4, N], F32)
+        quarters = [slice(q * QUARTER, (q + 1) * QUARTER) for q in range(4)]
+        sc = []
+
+        def by_rows(ap):
+            return ap.rearrange("p (j e) -> p j e", j=PACK)
+
+        def clearance(q):
+            s = bank("sc%d" % q, [P, PACK, QUARTER], "b%d" % q)
+            sc.append(s)
+            for j in range(PACK):
+                nc.tensor.matmul_mx(
+                    out=s[:, j, :],
+                    lhsT=hid_codes[:, quarters[j]].bitcast(FP8X4),
+                    lhsT_scale=hid_sc[:, quarters[j]],
+                    rhs=hid2_codes[:, quarters[q]].bitcast(FP8X4),
+                    rhs_scale=hid2_sc[:, quarters[q]],
+                    start=True,
+                    stop=True,
+                )
+            mag = sbuf("mag%d" % q, [P, PACK, QUARTER], F32)
+            nc.scalar.activation(out=mag[:], in_=s[:], func=ACT.Abs)
+            nc.vector.scalar_tensor_tensor(
+                out=clr[:, :, quarters[q]],
+                in0=mag[:],
+                scalar=0.1,
+                in1=radg[:, quarters[q]].unsqueeze(1).to_broadcast([P, PACK, QUARTER]),
+                op0=ALU.add,
+                op1=ALU.subtract,
+            )
+
+        def exponential(q):
+            floored = sbuf("floored%d" % q, [P, PACK, QUARTER], F32)
+            nc.vector.tensor_scalar(
+                out=floored[:], in0=clr[:, :, quarters[q]], scalar1=CLR_FLOOR, scalar2=None, op0=ALU.max
+            )
+            nc.scalar.activation(out=by_rows(expo[:, q, :]), in_=floored[:], func=ACT.Exp, scale=-2.0)
+
+        clearance(0)
+        for q in range(1, 4):
+            clearance(q)
+            exponential(q - 1)
+        exponential(3)
+
+        logs = sbuf("logs", [P, 4, N], F32, tag="floored3")
+        for q in range(4):
+            nc.scalar.activation(out=logs[:, q, :], in_=expo[:, q, :], func=ACT.Ln, bias=1.0)
+
+        nxt = [sbuf("nxt0", [P, PACK, HALF], F32), sbuf("nxt1", [P, PACK, HALF], F32, tag="expo")]
+        for j in range(PACK):
+            nc.vector.tensor_copy(out=nxt[0][:, j, :], in_=clr[:, j, :].indirect(nxo_t[:, 0:16]))
+        for j in range(PACK):
+            nc.scalar.activation(out=nxt[1][:, j, :], in_=clr[:, j, :].indirect(nxo_t[:, 16:32]), func=ACT.Copy)
+
+        out_rows = out_0.rearrange("(p j) e -> p j e", j=PACK)
+        out_words = out_1[0].rearrange("p e r -> p (e r)").bitcast(I32)
+        res_sc = sbuf("res_sc", [P, N], U8)
+        res_bf = sbuf("res_bf", [P, N * PACK], BF16)
+        pen, prod, res = {}, {}, {}
+
+        def penalty(q):
+            pen[q] = sbuf("pen%d" % q, [P, PACK, QUARTER], F32)
+            nc.vector.scalar_tensor_tensor(
+                out=pen[q][:], in0=clr[:, :, quarters[q]], scalar=-2.0, in1=by_rows(logs[:, q, :]), op0=ALU.mult, op1=ALU.max
+            )
+
+        def product(q):
+            prod[q] = sbuf("prod%d" % q, [P, PACK, QUARTER], F32)
+            nc.vector.tensor_tensor(out=prod[q][:], in0=sc[q][:], in1=pen[q][:], op=ALU.mult)
+
+        def result(q):
+            res[q] = sbuf("res%d" % q, [P, PACK, QUARTER], F32)
+            nc.vector.scalar_tensor_tensor(
+                out=res[q][:],
+                in0=nxt[q // 2][:, :, quarters[q % 2]],
+                scalar=-0.3,
+                in1=prod[q][:],
+                op0=ALU.mult,
+                op1=ALU.add,
+            )
+            nc.sync.dma_start(out=out_rows[:, :, quarters[q]], in_=res[q][:])
+
+        def interleave(q, copy):
+            copy(
+                out=res_bf[:, q * N : (q + 1) * N].rearrange("p (c i j) -> p c j i", i=4, j=PACK),
+                in_=res[q][:].rearrange("p j (c i) -> p c j i", i=4),
+            )
+
+        def planes(name, first, last, tag):
+            cols = slice(first * QUARTER, last * QUARTER)
+            codes = sbuf(name, [P, (last - first) * QUARTER], U32, tag=tag)
+            nc.vector.quantize_mx(out=codes[:].bitcast(FP8X4), scales=res_sc[:, cols], in_=res_bf[:, first * N : last * N])
+            nc.scalar.dma_start(out=out_words[:, cols], in_=codes[:].bitcast(I32))
+
+        stages = (penalty, product, result)
+        for step in range(4 + len(stages) - 1):
+            for k in range(len(stages)):
+                if 0 <= step - k < 4:
+                    stages[k](step - k)
+            if 2 <= step < 5:
+                interleave(step - 2, nc.scalar.copy)
+        planes("codes_head", 0, 3, "prod3")
+        interleave(3, nc.vector.tensor_copy)
+        planes("codes_tail", 3, 4, None)
+        for q in range(4):
+            queue = nc.sync if q % 2 else nc.scalar
+            queue.dma_start(
+                out=out_2[0, 4 * q : 4 * q + 4, :].bitcast(I32), in_=res_sc[32 * q : 32 * q + 4, :].bitcast(I32)
+            )

@@ -23,6 +23,7 @@ HALF = N // 2
 QUARTER = N // 4
 PAD = 16
 FUSED = 3
+LATE = 4
 CLR_FLOOR = -15.0
 
 FLOPS = 4 * 2 * N * N * N
@@ -50,80 +51,101 @@ def tile_picked_ycollid_way_po_kernel(
 
         def load_scale_rows(queue, dst, src):
             for q in range(4):
-                queue.dma_start(out=dst[32 * q : 32 * q + 4, :].bitcast(I32), in_=src[0, 4 * q : 4 * q + 4, :].bitcast(I32))
+                queue.dma_start(out=dst[32 * q : 32 * q + 4, :].bitcast(I32), in_=src[4 * q : 4 * q + 4, :].bitcast(I32))
 
         def load_words(dst, src):
             nc.sync.dma_start(out=dst[:].bitcast(I32), in_=src[0].rearrange("p n r -> p (n r)").bitcast(I32))
 
-        e_sc_tab = sbuf("e_sc_tab", [P, T_OBST], U8)
         x_sc_tab = sbuf("x_sc_tab", [P, T_LINKS], U8)
-        w3_sc_raw = sbuf("w3_sc_raw", [P, N], U8)
-        w21_sc_raw = sbuf("w21_sc_raw", [P, 2 * N], U8)
         unit_rows = sbuf("unit_rows", [P, P], F32)
-        nc.gpsimd.memset(w3_sc_raw[:].bitcast(I32), 0)
-        for t in (e_sc_tab, x_sc_tab, w21_sc_raw):
-            nc.vector.memset(t[:].bitcast(I32), 0)
-        nc.vector.memset(unit_rows[:], 0.0)
+        warm = sbuf("warm", [P, 3], F32)
+        nc.vector.memset(x_sc_tab[:].bitcast(I32), 0)
+        nc.vector.memset(warm[:, 2:3], 0.0)
+        ident = sbuf("ident", [P, P], F32)
+        nc.gpsimd.memset(ident[:], 0.0)
+        nc.gpsimd.memset(unit_rows[:], 0.0)
+        make_identity(nc, ident[:], nomemset=True)
 
-        load_scale_rows(nc.gpsimd, w3_sc_raw, w3_scales)
-        for i, src in enumerate((unit2, unit)):
-            nc.gpsimd.dma_start(
-                out=unit_rows[4 * i : 4 * i + 4, :].rearrange("t (b r) -> t b r", r=8),
-                in_=src.rearrange("(b t r) o -> t b (r o)", t=4, r=8),
+        def load_unit_rows(queue):
+            for i, src in enumerate((unit2, unit)):
+                queue.dma_start(
+                    out=unit_rows[4 * i : 4 * i + 4, :].rearrange("t (b r) -> t b r", r=8),
+                    in_=src.rearrange("(b t r) o -> t b (r o)", t=4, r=8),
+                )
+
+        rad_cols = sbuf("rad_cols", [P, T_OBST // P], F32)
+        w_sc_rows = sbuf("w_sc_rows", [16, 3 * N], U8)
+        w_sc_dealt = sbuf("w_sc_dealt", [16, 3 * N], U8)
+        w_sc = sbuf("w_sc", [P, 3 * N], U8)
+
+        def load_weight_scales(queue):
+            for i, src in enumerate((w3_scales, w2_scales, w1_scales)):
+                queue.dma_start(out=w_sc_rows[:, i * N : (i + 1) * N].bitcast(I32), in_=src[0].bitcast(I32))
+            nc.vector.tensor_copy(
+                out=w_sc_dealt[:].bitcast(I32).rearrange("p (w t b r) -> p w t b r", w=3, t=4, r=2),
+                in_=w_sc_rows[:].bitcast(I32).rearrange("p (w b t r) -> p w t b r", w=3, t=4, r=2),
             )
 
         w3_raw = sbuf("w3_raw", [P, 1, 2 * N // 4], I32)
         w21_raw = sbuf("w21_raw", [P, 2, 2 * N // 4], I32)
-        obs_t = load_list("obs_t", obs_)
         e_tab = sbuf("e_tab", [P, T_OBST], U32)
-        load_words(e_tab, e_words)
-        nc.sync.dma_start(out=w3_raw[:, 0, :], in_=w3_words[0].bitcast(I32))
-        load_scale_rows(nc.sync, e_sc_tab, e_scales)
-        offs_t = load_list("offs_t", offs)
         x_tab = sbuf("x_tab", [P, T_LINKS], U32)
+        load_unit_rows(nc.gpsimd)
+        nc.sync.dma_start(out=rad_cols[:], in_=rad[0, :].rearrange("(p m) -> p m", p=P))
+        load_weight_scales(nc.sync)
+        offs_t = load_list("offs_t", offs)
         load_words(x_tab, x_words)
-        load_scale_rows(nc.sync, x_sc_tab, x_scales)
+        load_scale_rows(nc.sync, x_sc_tab, x_scales[0])
+        load_words(e_tab, e_words)
         nc.sync.dma_start(out=w21_raw[:, 0, :], in_=w2_words[0].bitcast(I32))
         nc.sync.dma_start(out=w21_raw[:, 1, :], in_=w1_words[0].bitcast(I32))
+        load_scale_rows(nc.sync, w_sc, w_sc_dealt)
+        obs_t = load_list("obs_t", obs_)
+        e_sc_tab = sbuf("e_sc_tab", [P, T_OBST], U8, tag="w_sc_rows")
+        nc.vector.memset(e_sc_tab[:].bitcast(I32), 0)
+        load_scale_rows(nc.sync, e_sc_tab, e_scales[0])
+        nc.sync.dma_start(out=w3_raw[:, 0, :], in_=w3_words[0].bitcast(I32))
         par_t = load_list("par_t", par)
-        load_scale_rows(nc.sync, w21_sc_raw[:, 0:N], w2_scales)
-        load_scale_rows(nc.sync, w21_sc_raw[:, N : 2 * N], w1_scales)
         nxo_t = load_list("nxo_t", nxo)
 
-        def deal_weights(engine, name, count, raw, sc_raw):
-            words = sbuf(name, [P, count * 2 * N], U8)
-            scales = sbuf(name + "_sc", [P, count * N], U8)
-            engine.tensor_copy(
+        def deal_words(name, count, raw, tag):
+            words = sbuf(name, [P, count * 2 * N], U8, tag=tag)
+            nc.vector.tensor_copy(
                 out=words[:].bitcast(I32).rearrange("p (w t b r) -> p w t b r", w=count, t=4, r=4),
                 in_=raw[:].rearrange("p w (b t r) -> p w t b r", t=4, r=4),
             )
-            engine.tensor_copy(
-                out=scales[:].bitcast(I32).rearrange("p (w t b r) -> p w t b r", w=count, t=4, r=2),
-                in_=sc_raw[:].bitcast(I32).rearrange("p (w b t r) -> p w t b r", w=count, t=4, r=2),
-            )
-            return words, scales
+            return words
 
-        e_codes = sbuf("e_codes", [P, N], U32)
-        e_sc = sbuf("e_sc", [P, N], U8)
-        nc.vector.tensor_copy(out=e_codes[:], in_=e_tab[:].indirect(obs_t[:]))
-        nc.vector.tensor_copy(out=e_sc[:], in_=e_sc_tab[:].indirect(obs_t[:]))
-        w3, w3_sc = deal_weights(nc.gpsimd, "w3", 1, w3_raw, w3_sc_raw)
-        rad_tab = sbuf("rad_tab", [P, T_OBST], F32, tag="e_tab")
-        nc.sync.dma_start(out=rad_tab[:], in_=rad)
+        nc.scalar.activation(out=warm[:, 0:1], in_=warm[:, 2:3], func=ACT.Gelu_apprx_tanh)
+        rad_tab = sbuf("rad_tab", [P, T_OBST], F32)
+        for g in range(2):
+            rad_ps = bank("rad_ps%d" % g, [P, 4, P], "a%d" % g)
+            for m in range(4):
+                nc.tensor.transpose(rad_ps[:, m, :], rad_cols[:, 4 * g + m : 4 * g + m + 1].to_broadcast([P, P]), ident[:])
+            nc.scalar.copy(
+                out=rad_tab[:].rearrange("p (n m) -> p n m", m=8)[:, :, 4 * g : 4 * g + 4],
+                in_=rad_ps[:].rearrange("p m n -> p n m"),
+            )
+        radg = sbuf("radg", [P, N], F32)
+        nc.scalar.activation(out=radg[:], in_=rad_tab[:].indirect(obs_t[:]), func=ACT.Copy)
+
+        unit_ps = bank("unit_ps", [P, P], "a0")
+        nc.tensor.transpose(unit_ps[:], unit_rows[:], ident[:])
+        units = sbuf("units", [P, 8], F32)
+        unit06 = sbuf("unit06", [P, 4], F32)
+        nc.scalar.copy(out=units[:], in_=unit_ps[:, 0:8])
+        nc.scalar.activation(out=unit06[:], in_=unit_ps[:, 4:8], func=ACT.Copy, scale=0.6)
+
         x_codes = sbuf("x_codes", [P, N], U32)
         x_sc = sbuf("x_sc", [P, N], U8)
         nc.vector.tensor_copy(out=x_codes[:], in_=x_tab[:].indirect(offs_t[:]))
         nc.vector.tensor_copy(out=x_sc[:], in_=x_sc_tab[:].indirect(offs_t[:]))
-        w21, w21_sc = deal_weights(nc.vector, "w21", 2, w21_raw, w21_sc_raw)
-
-        ident = sbuf("ident", [P, P], F32, tag="w3_sc_raw")
-        make_identity(nc, ident[:])
-        unit_ps = bank("unit_ps", [P, P], "b3")
-        nc.tensor.transpose(unit_ps[:], unit_rows[:], ident[:])
-        units = sbuf("units", [P, 8], F32, tag="x_tab")
-        unit06 = sbuf("unit06", [P, 4], F32)
-        nc.vector.tensor_copy(out=units[:], in_=unit_ps[:, 0:8])
-        nc.gpsimd.tensor_scalar(out=unit06[:], in0=units[:, 4:8], scalar1=0.6, scalar2=None, op0=ALU.mult)
+        w21, w21_sc = deal_words("w21", 2, w21_raw, "x_tab"), w_sc[:, N:]
+        e_codes = sbuf("e_codes", [P, N], U32, tag="w21_raw")
+        e_sc = sbuf("e_sc", [P, N], U8)
+        nc.vector.tensor_copy(out=e_codes[:], in_=e_tab[:].indirect(obs_t[:]))
+        nc.vector.tensor_copy(out=e_sc[:], in_=e_sc_tab[:].indirect(obs_t[:]))
+        w3, w3_sc = deal_words("w3", 1, w3_raw, "e_tab"), w_sc[:, :N]
 
         def weight_product(out, words, scales, col0, codes, code_scales):
             nc.tensor.matmul_mx(
@@ -135,24 +157,6 @@ def tile_picked_ycollid_way_po_kernel(
                 start=True,
                 stop=True,
             )
-
-        hid2_bf = sbuf("hid2_bf", [P, N * PACK], BF16, tag="w21_sc_raw")
-        for q in range(4):
-            cols = slice(q * QUARTER, (q + 1) * QUARTER)
-            ye = bank("ye%d" % q, [P, PACK, QUARTER], "a%d" % q)
-            for t in range(PACK):
-                weight_product(ye[:, t, :], w3, w3_sc, t * P, e_codes[:, cols], e_sc[:, cols])
-            obst = sbuf("obst%d" % q, [P, QUARTER, PACK], F32)
-            nc.scalar.activation(out=obst[:], in_=ye[:].rearrange("p t n -> p n t"), func=ACT.Gelu_apprx_tanh)
-            nc.vector.tensor_tensor(
-                out=hid2_bf[:, q * N : (q + 1) * N].rearrange("p (n t) -> p n t", t=PACK),
-                in0=obst[:],
-                in1=units[:, 0:4].unsqueeze(1).to_broadcast([P, QUARTER, PACK]),
-                op=ALU.mult,
-            )
-        hid2_codes = sbuf("hid2_codes", [P, N], U32)
-        hid2_sc = sbuf("hid2_sc", [P, N], U8)
-        nc.vector.quantize_mx(out=hid2_codes[:].bitcast(FP8X4), scales=hid2_sc[:], in_=hid2_bf[:])
 
         hid = sbuf("hid", [P, PACK, N], F32)
         for t in range(PACK):
@@ -172,8 +176,6 @@ def tile_picked_ycollid_way_po_kernel(
                 nc.vector.scalar_tensor_tensor(
                     out=hid[:, t, :], in0=y[:], scalar=units[:, 4 + t : 5 + t], in1=part[:], op0=ALU.mult, op1=ALU.add
                 )
-        radg = sbuf("radg", [P, N], F32, tag="yv_s3")
-        nc.scalar.activation(out=radg[:], in_=rad_tab[:].indirect(obs_t[:]), func=ACT.Copy)
 
         hid_bf = sbuf("hid_bf", [P, N * PACK], BF16)
         nc.vector.tensor_copy(
@@ -184,6 +186,41 @@ def tile_picked_ycollid_way_po_kernel(
         hid_sc = sbuf("hid_sc", [P, N], U8)
         nc.vector.quantize_mx(out=hid_codes[:].bitcast(FP8X4), scales=hid_sc[:], in_=hid_bf[:])
 
+        hid2_codes = sbuf("hid2_codes", [P, N], U32)
+        hid2_sc = sbuf("hid2_sc", [P, N], U8)
+        obst, hid2_bf = {}, {}
+        obst_all = sbuf("obst_all", [P, 4, QUARTER, PACK], F32, tag="yv_s3")
+
+        def obstacle(q):
+            cols = slice(q * QUARTER, (q + 1) * QUARTER)
+            ye = bank("ye%d" % q, [P, PACK, QUARTER], "b%d" % q)
+            for t in range(PACK):
+                weight_product(ye[:, t, :], w3, w3_sc, t * P, e_codes[:, cols], e_sc[:, cols])
+            obst[q] = obst_all[:, q]
+            nc.scalar.activation(out=obst[q][:], in_=ye[:].rearrange("p t n -> p n t"), func=ACT.Gelu_apprx_tanh)
+            hid2_bf[q] = sbuf("hid2_bf%d" % q, [P, QUARTER, PACK], BF16)
+            nc.vector.tensor_tensor(
+                out=hid2_bf[q][:],
+                in0=obst[q][:],
+                in1=units[:, 0:4].unsqueeze(1).to_broadcast([P, QUARTER, PACK]),
+                op=ALU.mult,
+            )
+
+        def obstacle_codes(q):
+            cols = slice(q * QUARTER, (q + 1) * QUARTER)
+            nc.vector.quantize_mx(
+                out=hid2_codes[:, cols].bitcast(FP8X4),
+                scales=hid2_sc[:, cols],
+                in_=hid2_bf[q][:].rearrange("p n t -> p (n t)"),
+            )
+
+        obstacle(0)
+        for q in range(1, 4):
+            obstacle(q)
+            obstacle_codes(q - 1)
+        obstacle_codes(3)
+        nc.scalar.activation(out=warm[:, 1:2], in_=obst[3][:, 0, 0:1], func=ACT.Exp)
+
         clr = sbuf("clr", [P, PACK, N], F32)
         expo = sbuf("expo", [P, 4, N], F32)
         quarters = [slice(q * QUARTER, (q + 1) * QUARTER) for q in range(4)]
@@ -193,7 +230,7 @@ def tile_picked_ycollid_way_po_kernel(
             return ap.rearrange("p (j e) -> p j e", j=PACK)
 
         def clearance(q):
-            s = bank("sc%d" % q, [P, PACK, QUARTER], "b%d" % q)
+            s = bank("sc%d" % q, [P, PACK, QUARTER], "a%d" % q)
             sc.append(s)
             for j in range(PACK):
                 nc.tensor.matmul_mx(
@@ -237,7 +274,11 @@ def tile_picked_ycollid_way_po_kernel(
         for j in range(PACK):
             nc.vector.tensor_copy(out=nxt[0][:, j, :], in_=clr[:, j, :].indirect(nxo_t[:, 0:16]))
         for j in range(PACK):
-            nc.scalar.activation(out=nxt[1][:, j, :], in_=clr[:, j, :].indirect(nxo_t[:, 16:32]), func=ACT.Copy)
+            window = clr[:, j, :].indirect(nxo_t[:, 16:32])
+            if j < PACK - LATE:
+                nc.vector.tensor_copy(out=nxt[1][:, j, :], in_=window)
+            else:
+                nc.scalar.activation(out=nxt[1][:, j, :], in_=window, func=ACT.Copy)
 
         out_rows = out_0.rearrange("(p j) e -> p j e", j=PACK)
         out_words = out_1[0].rearrange("p e r -> p (e r)").bitcast(I32)

@@ -21,10 +21,10 @@ T_LINKS = 2048
 T_OBST = 1024
 HALF = N // 2
 QUARTER = N // 4
-PAD = 16
-FUSED = 3
-LATE = 4
-CLR_FLOOR = -15.0
+ON_VECTOR = 2
+NEXT_ON_VECTOR = 1
+SPLIT = 80
+EXP_CAP = 2.0**43
 
 FLOPS = 4 * 2 * N * N * N
 
@@ -59,12 +59,11 @@ def tile_picked_ycollid_way_po_kernel(
         x_sc_tab = sbuf("x_sc_tab", [P, T_LINKS], U8)
         unit_rows = sbuf("unit_rows", [P, P], F32)
         warm = sbuf("warm", [P, 3], F32)
+        nc.vector.memset(unit_rows[:], 0.0)
         nc.vector.memset(x_sc_tab[:].bitcast(I32), 0)
         nc.vector.memset(warm[:, 2:3], 0.0)
         ident = sbuf("ident", [P, P], F32)
-        nc.gpsimd.memset(ident[:], 0.0)
-        nc.gpsimd.memset(unit_rows[:], 0.0)
-        make_identity(nc, ident[:], nomemset=True)
+        make_identity(nc, ident[:])
 
         def load_unit_rows(queue):
             for i, src in enumerate((unit2, unit)):
@@ -90,11 +89,11 @@ def tile_picked_ycollid_way_po_kernel(
         w21_raw = sbuf("w21_raw", [P, 2, 2 * N // 4], I32)
         e_tab = sbuf("e_tab", [P, T_OBST], U32)
         x_tab = sbuf("x_tab", [P, T_LINKS], U32)
-        load_unit_rows(nc.gpsimd)
         nc.sync.dma_start(out=rad_cols[:], in_=rad[0, :].rearrange("(p m) -> p m", p=P))
         load_weight_scales(nc.sync)
         offs_t = load_list("offs_t", offs)
         load_words(x_tab, x_words)
+        load_unit_rows(nc.sync)
         load_scale_rows(nc.sync, x_sc_tab, x_scales[0])
         load_words(e_tab, e_words)
         nc.sync.dma_start(out=w21_raw[:, 0, :], in_=w2_words[0].bitcast(I32))
@@ -122,9 +121,12 @@ def tile_picked_ycollid_way_po_kernel(
             rad_ps = bank("rad_ps%d" % g, [P, 4, P], "a%d" % g)
             for m in range(4):
                 nc.tensor.transpose(rad_ps[:, m, :], rad_cols[:, 4 * g + m : 4 * g + m + 1].to_broadcast([P, P]), ident[:])
-            nc.scalar.copy(
+            nc.scalar.activation(
                 out=rad_tab[:].rearrange("p (n m) -> p n m", m=8)[:, :, 4 * g : 4 * g + 4],
                 in_=rad_ps[:].rearrange("p m n -> p n m"),
+                func=ACT.Copy,
+                scale=-0.5,
+                bias=0.05,
             )
         radg = sbuf("radg", [P, N], F32)
         nc.scalar.activation(out=radg[:], in_=rad_tab[:].indirect(obs_t[:]), func=ACT.Copy)
@@ -158,33 +160,37 @@ def tile_picked_ycollid_way_po_kernel(
                 stop=True,
             )
 
-        hid = sbuf("hid", [P, PACK, N], F32)
+        parents = []
         for t in range(PACK):
             yv = bank("yv%d" % t, [P, N], "b%d" % t)
             weight_product(yv[:], w21, w21_sc, t * P, x_codes[:], x_sc[:])
+            yv_s = sbuf("yv_s%d" % t, [P, N], F32)
+            nc.scalar.activation(out=yv_s[:], in_=yv[:], func=ACT.Copy, scale=unit06[:, t : t + 1])
+            parents.append(yv_s)
+        hid = sbuf("hid", [P, PACK, N], F32, tag="w_sc_rows")
+        vp_v = sbuf("vp_v", [P, ON_VECTOR, N], F32, tag="w3_raw")
+        vp_s = sbuf("vp_s", [P, PACK - ON_VECTOR, N], F32)
+        for t in range(PACK):
             y = bank("y%d" % t, [P, N], "a%d" % t)
             weight_product(y[:], w21, w21_sc, N + t * P, x_codes[:], x_sc[:])
-            yv_s = sbuf("yv_s%d" % t, [P, N + PAD], F32)
-            nc.vector.memset(yv_s[:, N:], 0.0)
-            nc.scalar.activation(out=yv_s[:, :N], in_=yv[:], func=ACT.Copy, scale=unit06[:, t : t + 1])
-            part = sbuf("part%d" % t, [P, N], F32)
-            if t < FUSED:
-                nc.scalar.activation(out=part[:], in_=y[:], func=ACT.Copy, scale=units[:, 4 + t : 5 + t])
-                nc.vector.tensor_tensor(out=hid[:, t, :], in0=yv_s[:].indirect(par_t[:]), in1=part[:], op=ALU.add)
-            else:
-                nc.scalar.activation(out=part[:], in_=yv_s[:].indirect(par_t[:]), func=ACT.Copy)
-                nc.vector.scalar_tensor_tensor(
-                    out=hid[:, t, :], in0=y[:], scalar=units[:, 4 + t : 5 + t], in1=part[:], op0=ALU.mult, op1=ALU.add
-                )
+            vp = vp_v[:, t, :] if t < ON_VECTOR else vp_s[:, t - ON_VECTOR, :]
+            for h in range(2):
+                window = parents[t][:].indirect(par_t[:, 16 * h : 16 * h + 16])
+                if t < ON_VECTOR:
+                    nc.vector.tensor_copy(out=vp[:, h * HALF : (h + 1) * HALF], in_=window)
+                else:
+                    nc.scalar.activation(out=vp[:, h * HALF : (h + 1) * HALF], in_=window, func=ACT.Copy)
+            nc.vector.scalar_tensor_tensor(
+                out=hid[:, t, :], in0=y[:], scalar=units[:, 4 + t : 5 + t], in1=vp, op0=ALU.mult, op1=ALU.add
+            )
 
         hid_bf = sbuf("hid_bf", [P, N * PACK], BF16)
         nc.vector.tensor_copy(
-            out=hid_bf[:].rearrange("p (j m t) -> p m t j", j=PACK, t=PACK),
-            in_=hid[:].rearrange("p t (m j) -> p m t j", j=PACK),
+            out=hid_bf[:].rearrange("p (j m t) -> p m j t", j=PACK, t=PACK)[:, :SPLIT],
+            in_=hid[:].rearrange("p t (m j) -> p m j t", j=PACK)[:, :SPLIT],
         )
         hid_codes = sbuf("hid_codes", [P, N], U32)
         hid_sc = sbuf("hid_sc", [P, N], U8)
-        nc.vector.quantize_mx(out=hid_codes[:].bitcast(FP8X4), scales=hid_sc[:], in_=hid_bf[:])
 
         hid2_codes = sbuf("hid2_codes", [P, N], U32)
         hid2_sc = sbuf("hid2_sc", [P, N], U8)
@@ -215,14 +221,22 @@ def tile_picked_ycollid_way_po_kernel(
             )
 
         obstacle(0)
-        for q in range(1, 4):
+        obstacle(1)
+        obstacle_codes(0)
+        nc.scalar.copy(
+            out=hid_bf[:].rearrange("p (j m t) -> p m j t", j=PACK, t=PACK)[:, SPLIT:],
+            in_=hid[:].rearrange("p t (m j) -> p m j t", j=PACK)[:, SPLIT:],
+        )
+        nc.vector.quantize_mx(out=hid_codes[:].bitcast(FP8X4), scales=hid_sc[:], in_=hid_bf[:])
+        for q in range(2, 4):
             obstacle(q)
             obstacle_codes(q - 1)
         obstacle_codes(3)
         nc.scalar.activation(out=warm[:, 1:2], in_=obst[3][:, 0, 0:1], func=ACT.Exp)
 
         clr = sbuf("clr", [P, PACK, N], F32)
-        expo = sbuf("expo", [P, 4, N], F32)
+        expo_head = sbuf("expo_head", [P, 3, N], F32)
+        expo_tail = sbuf("expo_tail", [P, N], F32)
         quarters = [slice(q * QUARTER, (q + 1) * QUARTER) for q in range(4)]
         sc = []
 
@@ -242,43 +256,45 @@ def tile_picked_ycollid_way_po_kernel(
                     start=True,
                     stop=True,
                 )
+            base = radg[:, quarters[q]].unsqueeze(1).to_broadcast([P, PACK, QUARTER])
             mag = sbuf("mag%d" % q, [P, PACK, QUARTER], F32)
-            nc.scalar.activation(out=mag[:], in_=s[:], func=ACT.Abs)
-            nc.vector.scalar_tensor_tensor(
-                out=clr[:, :, quarters[q]],
-                in0=mag[:],
-                scalar=0.1,
-                in1=radg[:, quarters[q]].unsqueeze(1).to_broadcast([P, PACK, QUARTER]),
-                op0=ALU.add,
-                op1=ALU.subtract,
-            )
+            if q < 3:
+                nc.scalar.activation(out=mag[:], in_=s[:], func=ACT.Abs, scale=0.5)
+                nc.vector.tensor_tensor(out=clr[:, :, quarters[q]], in0=mag[:], in1=base, op=ALU.add)
+            else:
+                nc.vector.scalar_tensor_tensor(out=mag[:], in0=s[:], scalar=-0.5, in1=base, op0=ALU.mult, op1=ALU.add)
+                nc.vector.scalar_tensor_tensor(
+                    out=clr[:, :, quarters[q]], in0=s[:], scalar=0.0, in1=mag[:], op0=ALU.max, op1=ALU.add
+                )
 
         def exponential(q):
-            floored = sbuf("floored%d" % q, [P, PACK, QUARTER], F32)
-            nc.vector.tensor_scalar(
-                out=floored[:], in0=clr[:, :, quarters[q]], scalar1=CLR_FLOOR, scalar2=None, op0=ALU.max
-            )
-            nc.scalar.activation(out=by_rows(expo[:, q, :]), in_=floored[:], func=ACT.Exp, scale=-2.0)
+            dst = expo_head[:, q, :] if q < 3 else expo_tail[:]
+            nc.scalar.activation(out=by_rows(dst), in_=clr[:, :, quarters[q]], func=ACT.Exp, scale=-4.0)
 
-        clearance(0)
-        for q in range(1, 4):
-            clearance(q)
-            exponential(q - 1)
-        exponential(3)
-
-        logs = sbuf("logs", [P, 4, N], F32, tag="floored3")
         for q in range(4):
-            nc.scalar.activation(out=logs[:, q, :], in_=expo[:, q, :], func=ACT.Ln, bias=1.0)
+            clearance(q)
+        for q in range(4):
+            exponential(q)
 
-        nxt = [sbuf("nxt0", [P, PACK, HALF], F32), sbuf("nxt1", [P, PACK, HALF], F32, tag="expo")]
-        for j in range(PACK):
-            nc.vector.tensor_copy(out=nxt[0][:, j, :], in_=clr[:, j, :].indirect(nxo_t[:, 0:16]))
-        for j in range(PACK):
-            window = clr[:, j, :].indirect(nxo_t[:, 16:32])
-            if j < PACK - LATE:
-                nc.vector.tensor_copy(out=nxt[1][:, j, :], in_=window)
-            else:
-                nc.scalar.activation(out=nxt[1][:, j, :], in_=window, func=ACT.Copy)
+        capped = sbuf("capped", [P, 4, N], F32)
+        nc.vector.tensor_scalar(out=capped[:, :3, :], in0=expo_head[:], scalar1=EXP_CAP, scalar2=None, op0=ALU.min)
+        nc.vector.tensor_scalar(out=capped[:, 3, :], in0=expo_tail[:], scalar1=EXP_CAP, scalar2=None, op0=ALU.min)
+        logs = sbuf("logs", [P, 4, N], F32)
+        for q in range(4):
+            nc.scalar.activation(out=logs[:, q, :], in_=capped[:, q, :], func=ACT.Ln, bias=1.0)
+
+        nxt = [sbuf("nxt0", [P, PACK, QUARTER], F32)]
+        if NEXT_ON_VECTOR == 2:
+            nxt.append(sbuf("nxt1", [P, PACK, QUARTER], F32, tag="expo_tail"))
+        late = sbuf("nxt_late", [P, 4 - NEXT_ON_VECTOR, PACK, QUARTER], F32, tag="capped")
+        nxt = [t[:] for t in nxt] + [late[:, i] for i in range(4 - NEXT_ON_VECTOR)]
+        for q in range(4):
+            for j in range(PACK):
+                window = clr[:, j, :].indirect(nxo_t[:, 8 * q : 8 * q + 8])
+                if q < NEXT_ON_VECTOR:
+                    nc.vector.tensor_copy(out=nxt[q][:, j, :], in_=window)
+                else:
+                    nc.scalar.activation(out=nxt[q][:, j, :], in_=window, func=ACT.Copy)
 
         out_rows = out_0.rearrange("(p j) e -> p j e", j=PACK)
         out_words = out_1[0].rearrange("p e r -> p (e r)").bitcast(I32)
@@ -289,7 +305,7 @@ def tile_picked_ycollid_way_po_kernel(
         def penalty(q):
             pen[q] = sbuf("pen%d" % q, [P, PACK, QUARTER], F32)
             nc.vector.scalar_tensor_tensor(
-                out=pen[q][:], in0=clr[:, :, quarters[q]], scalar=-2.0, in1=by_rows(logs[:, q, :]), op0=ALU.mult, op1=ALU.max
+                out=pen[q][:], in0=clr[:, :, quarters[q]], scalar=-4.0, in1=by_rows(logs[:, q, :]), op0=ALU.mult, op1=ALU.max
             )
 
         def product(q):
@@ -300,8 +316,8 @@ def tile_picked_ycollid_way_po_kernel(
             res[q] = sbuf("res%d" % q, [P, PACK, QUARTER], F32)
             nc.vector.scalar_tensor_tensor(
                 out=res[q][:],
-                in0=nxt[q // 2][:, :, quarters[q % 2]],
-                scalar=-0.3,
+                in0=nxt[q],
+                scalar=-0.6,
                 in1=prod[q][:],
                 op0=ALU.mult,
                 op1=ALU.add,

from contextlib import ExitStack

import concourse.mybir as mybir
from concourse.masks import make_identity

F32 = mybir.dt.float32
BF16 = mybir.dt.bfloat16
I32 = mybir.dt.int32
U32 = mybir.dt.uint32
U16 = mybir.dt.uint16
U8 = mybir.dt.uint8
FP8X4 = mybir.dt.float8_e4m3fn_x4
FP4X4 = mybir.dt.float4_e2m1fn_x4
ALU = mybir.AluOpType
ACT = mybir.ActivationFunctionType

P = 128
PACK = 4
N = 512
T_LINKS = 2048
T_OBST = 1024
HALF = N // 2
QUARTER = N // 4
ON_VECTOR = 2
NEXT_ON_VECTOR = 1
SPLIT = 80
EXP_CAP = 2.0**43

FLOPS = 4 * 2 * N * N * N


def tile_picked_ycollid_way_po_kernel(
    tc, x_words, x_scales, w1_words, w1_scales, w2_words, w2_scales, e_words, e_scales,
    w3_words, w3_scales, unit, unit2, rad, offs, obs_, par, nxo, out_0, out_1, out_2,
):
    nc = tc.nc
    with ExitStack() as ctx:
        sb = ctx.enter_context(tc.tile_pool(name="sb", bufs=1))
        psum = ctx.enter_context(tc.psum_pool(name="psum", bufs=1))

        def sbuf(name, shape, dtype, tag=None):
            return sb.tile(shape, dtype, name=name, tag=tag or name, align_bytes=64)

        def bank(name, shape, tag):
            return psum.tile(shape, F32, name=name, tag=tag)

        def load_list(name, src):
            t = sbuf(name, [P, N // 16], U16)
            nc.sync.dma_start(t[:], src)
            return t

        def load_scale_rows(queue, dst, src):
            for q in range(4):
                queue.dma_start(out=dst[32 * q : 32 * q + 4, :].bitcast(I32), in_=src[4 * q : 4 * q + 4, :].bitcast(I32))

        def load_words(dst, src):
            nc.sync.dma_start(out=dst[:].bitcast(I32), in_=src[0].rearrange("p n r -> p (n r)").bitcast(I32))

        x_sc_tab = sbuf("x_sc_tab", [P, T_LINKS], U8)
        unit_rows = sbuf("unit_rows", [P, P], F32)
        warm = sbuf("warm", [P, 3], F32)
        nc.vector.memset(unit_rows[:], 0.0)
        nc.vector.memset(x_sc_tab[:].bitcast(I32), 0)
        nc.vector.memset(warm[:, 2:3], 0.0)
        ident = sbuf("ident", [P, P], F32)
        make_identity(nc, ident[:])

        def load_unit_rows(queue):
            for i, src in enumerate((unit2, unit)):
                queue.dma_start(
                    out=unit_rows[4 * i : 4 * i + 4, :].rearrange("t (b r) -> t b r", r=8),
                    in_=src.rearrange("(b t r) o -> t b (r o)", t=4, r=8),
                )

        rad_cols = sbuf("rad_cols", [P, T_OBST // P], F32)
        w_sc_rows = sbuf("w_sc_rows", [16, 3 * N], U8)
        w_sc_dealt = sbuf("w_sc_dealt", [16, 3 * N], U8)
        w_sc = sbuf("w_sc", [P, 3 * N], U8)

        def load_weight_scales(queue):
            for i, src in enumerate((w3_scales, w2_scales, w1_scales)):
                queue.dma_start(out=w_sc_rows[:, i * N : (i + 1) * N].bitcast(I32), in_=src[0].bitcast(I32))
            nc.vector.tensor_copy(
                out=w_sc_dealt[:].bitcast(I32).rearrange("p (w t b r) -> p w t b r", w=3, t=4, r=2),
                in_=w_sc_rows[:].bitcast(I32).rearrange("p (w b t r) -> p w t b r", w=3, t=4, r=2),
            )

        w3_raw = sbuf("w3_raw", [P, 1, 2 * N // 4], I32)
        w21_raw = sbuf("w21_raw", [P, 2, 2 * N // 4], I32)
        e_tab = sbuf("e_tab", [P, T_OBST], U32)
        x_tab = sbuf("x_tab", [P, T_LINKS], U32)
        nc.sync.dma_start(out=rad_cols[:], in_=rad[0, :].rearrange("(p m) -> p m", p=P))
        load_weight_scales(nc.sync)
        offs_t = load_list("offs_t", offs)
        load_words(x_tab, x_words)
        load_unit_rows(nc.sync)
        load_scale_rows(nc.sync, x_sc_tab, x_scales[0])
        load_words(e_tab, e_words)
        nc.sync.dma_start(out=w21_raw[:, 0, :], in_=w2_words[0].bitcast(I32))
        nc.sync.dma_start(out=w21_raw[:, 1, :], in_=w1_words[0].bitcast(I32))
        load_scale_rows(nc.sync, w_sc, w_sc_dealt)
        obs_t = load_list("obs_t", obs_)
        e_sc_tab = sbuf("e_sc_tab", [P, T_OBST], U8, tag="w_sc_rows")
        nc.vector.memset(e_sc_tab[:].bitcast(I32), 0)
        load_scale_rows(nc.sync, e_sc_tab, e_scales[0])
        nc.sync.dma_start(out=w3_raw[:, 0, :], in_=w3_words[0].bitcast(I32))
        par_t = load_list("par_t", par)
        nxo_t = load_list("nxo_t", nxo)

        def deal_words(name, count, raw, tag):
            words = sbuf(name, [P, count * 2 * N], U8, tag=tag)
            nc.vector.tensor_copy(
                out=words[:].bitcast(I32).rearrange("p (w t b r) -> p w t b r", w=count, t=4, r=4),
                in_=raw[:].rearrange("p w (b t r) -> p w t b r", t=4, r=4),
            )
            return words

        nc.scalar.activation(out=warm[:, 0:1], in_=warm[:, 2:3], func=ACT.Gelu_apprx_tanh)
        rad_tab = sbuf("rad_tab", [P, T_OBST], F32)
        for g in range(2):
            rad_ps = bank("rad_ps%d" % g, [P, 4, P], "a%d" % g)
            for m in range(4):
                nc.tensor.transpose(rad_ps[:, m, :], rad_cols[:, 4 * g + m : 4 * g + m + 1].to_broadcast([P, P]), ident[:])
            nc.scalar.activation(
                out=rad_tab[:].rearrange("p (n m) -> p n m", m=8)[:, :, 4 * g : 4 * g + 4],
                in_=rad_ps[:].rearrange("p m n -> p n m"),
                func=ACT.Copy,
                scale=-0.5,
                bias=0.05,
            )
        radg = sbuf("radg", [P, N], F32)
        nc.scalar.activation(out=radg[:], in_=rad_tab[:].indirect(obs_t[:]), func=ACT.Copy)

        unit_ps = bank("unit_ps", [P, P], "a0")
        nc.tensor.transpose(unit_ps[:], unit_rows[:], ident[:])
        units = sbuf("units", [P, 8], F32)
        unit06 = sbuf("unit06", [P, 4], F32)
        nc.scalar.copy(out=units[:], in_=unit_ps[:, 0:8])
        nc.scalar.activation(out=unit06[:], in_=unit_ps[:, 4:8], func=ACT.Copy, scale=0.6)

        x_codes = sbuf("x_codes", [P, N], U32)
        x_sc = sbuf("x_sc", [P, N], U8)
        nc.vector.tensor_copy(out=x_codes[:], in_=x_tab[:].indirect(offs_t[:]))
        nc.vector.tensor_copy(out=x_sc[:], in_=x_sc_tab[:].indirect(offs_t[:]))
        w21, w21_sc = deal_words("w21", 2, w21_raw, "x_tab"), w_sc[:, N:]
        e_codes = sbuf("e_codes", [P, N], U32, tag="w21_raw")
        e_sc = sbuf("e_sc", [P, N], U8)
        nc.vector.tensor_copy(out=e_codes[:], in_=e_tab[:].indirect(obs_t[:]))
        nc.vector.tensor_copy(out=e_sc[:], in_=e_sc_tab[:].indirect(obs_t[:]))
        w3, w3_sc = deal_words("w3", 1, w3_raw, "e_tab"), w_sc[:, :N]

        def weight_product(out, words, scales, col0, codes, code_scales):
            nc.tensor.matmul_mx(
                out=out,
                lhsT=words[:, 2 * col0 : 2 * (col0 + P)].bitcast(FP4X4),
                lhsT_scale=scales[:, col0 : col0 + P],
                rhs=codes.bitcast(FP8X4),
                rhs_scale=code_scales,
                start=True,
                stop=True,
            )

        parents = []
        for t in range(PACK):
            yv = bank("yv%d" % t, [P, N], "b%d" % t)
            weight_product(yv[:], w21, w21_sc, t * P, x_codes[:], x_sc[:])
            yv_s = sbuf("yv_s%d" % t, [P, N], F32)
            nc.scalar.activation(out=yv_s[:], in_=yv[:], func=ACT.Copy, scale=unit06[:, t : t + 1])
            parents.append(yv_s)
        hid = sbuf("hid", [P, PACK, N], F32, tag="w_sc_rows")
        vp_v = sbuf("vp_v", [P, ON_VECTOR, N], F32, tag="w3_raw")
        vp_s = sbuf("vp_s", [P, PACK - ON_VECTOR, N], F32)
        for t in range(PACK):
            y = bank("y%d" % t, [P, N], "a%d" % t)
            weight_product(y[:], w21, w21_sc, N + t * P, x_codes[:], x_sc[:])
            vp = vp_v[:, t, :] if t < ON_VECTOR else vp_s[:, t - ON_VECTOR, :]
            for h in range(2):
                window = parents[t][:].indirect(par_t[:, 16 * h : 16 * h + 16])
                if t < ON_VECTOR:
                    nc.vector.tensor_copy(out=vp[:, h * HALF : (h + 1) * HALF], in_=window)
                else:
                    nc.scalar.activation(out=vp[:, h * HALF : (h + 1) * HALF], in_=window, func=ACT.Copy)
            nc.vector.scalar_tensor_tensor(
                out=hid[:, t, :], in0=y[:], scalar=units[:, 4 + t : 5 + t], in1=vp, op0=ALU.mult, op1=ALU.add
            )

        hid_bf = sbuf("hid_bf", [P, N * PACK], BF16)
        nc.vector.tensor_copy(
            out=hid_bf[:].rearrange("p (j m t) -> p m j t", j=PACK, t=PACK)[:, :SPLIT],
            in_=hid[:].rearrange("p t (m j) -> p m j t", j=PACK)[:, :SPLIT],
        )
        hid_codes = sbuf("hid_codes", [P, N], U32)
        hid_sc = sbuf("hid_sc", [P, N], U8)

        hid2_codes = sbuf("hid2_codes", [P, N], U32)
        hid2_sc = sbuf("hid2_sc", [P, N], U8)
        obst, hid2_bf = {}, {}
        obst_all = sbuf("obst_all", [P, 4, QUARTER, PACK], F32, tag="yv_s3")

        def obstacle(q):
            cols = slice(q * QUARTER, (q + 1) * QUARTER)
            ye = bank("ye%d" % q, [P, PACK, QUARTER], "b%d" % q)
            for t in range(PACK):
                weight_product(ye[:, t, :], w3, w3_sc, t * P, e_codes[:, cols], e_sc[:, cols])
            obst[q] = obst_all[:, q]
            nc.scalar.activation(out=obst[q][:], in_=ye[:].rearrange("p t n -> p n t"), func=ACT.Gelu_apprx_tanh)
            hid2_bf[q] = sbuf("hid2_bf%d" % q, [P, QUARTER, PACK], BF16)
            nc.vector.tensor_tensor(
                out=hid2_bf[q][:],
                in0=obst[q][:],
                in1=units[:, 0:4].unsqueeze(1).to_broadcast([P, QUARTER, PACK]),
                op=ALU.mult,
            )

        def obstacle_codes(q):
            cols = slice(q * QUARTER, (q + 1) * QUARTER)
            nc.vector.quantize_mx(
                out=hid2_codes[:, cols].bitcast(FP8X4),
                scales=hid2_sc[:, cols],
                in_=hid2_bf[q][:].rearrange("p n t -> p (n t)"),
            )

        obstacle(0)
        obstacle(1)
        obstacle_codes(0)
        nc.scalar.copy(
            out=hid_bf[:].rearrange("p (j m t) -> p m j t", j=PACK, t=PACK)[:, SPLIT:],
            in_=hid[:].rearrange("p t (m j) -> p m j t", j=PACK)[:, SPLIT:],
        )
        nc.vector.quantize_mx(out=hid_codes[:].bitcast(FP8X4), scales=hid_sc[:], in_=hid_bf[:])
        for q in range(2, 4):
            obstacle(q)
            obstacle_codes(q - 1)
        obstacle_codes(3)
        nc.scalar.activation(out=warm[:, 1:2], in_=obst[3][:, 0, 0:1], func=ACT.Exp)

        clr = sbuf("clr", [P, PACK, N], F32)
        expo_head = sbuf("expo_head", [P, 3, N], F32)
        expo_tail = sbuf("expo_tail", [P, N], F32)
        quarters = [slice(q * QUARTER, (q + 1) * QUARTER) for q in range(4)]
        sc = []

        def by_rows(ap):
            return ap.rearrange("p (j e) -> p j e", j=PACK)

        def clearance(q):
            s = bank("sc%d" % q, [P, PACK, QUARTER], "a%d" % q)
            sc.append(s)
            for j in range(PACK):
                nc.tensor.matmul_mx(
                    out=s[:, j, :],
                    lhsT=hid_codes[:, quarters[j]].bitcast(FP8X4),
                    lhsT_scale=hid_sc[:, quarters[j]],
                    rhs=hid2_codes[:, quarters[q]].bitcast(FP8X4),
                    rhs_scale=hid2_sc[:, quarters[q]],
                    start=True,
                    stop=True,
                )
            base = radg[:, quarters[q]].unsqueeze(1).to_broadcast([P, PACK, QUARTER])
            mag = sbuf("mag%d" % q, [P, PACK, QUARTER], F32)
            if q < 3:
                nc.scalar.activation(out=mag[:], in_=s[:], func=ACT.Abs, scale=0.5)
                nc.vector.tensor_tensor(out=clr[:, :, quarters[q]], in0=mag[:], in1=base, op=ALU.add)
            else:
                nc.vector.scalar_tensor_tensor(out=mag[:], in0=s[:], scalar=-0.5, in1=base, op0=ALU.mult, op1=ALU.add)
                nc.vector.scalar_tensor_tensor(
                    out=clr[:, :, quarters[q]], in0=s[:], scalar=0.0, in1=mag[:], op0=ALU.max, op1=ALU.add
                )

        def exponential(q):
            dst = expo_head[:, q, :] if q < 3 else expo_tail[:]
            nc.scalar.activation(out=by_rows(dst), in_=clr[:, :, quarters[q]], func=ACT.Exp, scale=-4.0)

        for q in range(4):
            clearance(q)
        for q in range(4):
            exponential(q)

        capped = sbuf("capped", [P, 4, N], F32)
        nc.vector.tensor_scalar(out=capped[:, :3, :], in0=expo_head[:], scalar1=EXP_CAP, scalar2=None, op0=ALU.min)
        nc.vector.tensor_scalar(out=capped[:, 3, :], in0=expo_tail[:], scalar1=EXP_CAP, scalar2=None, op0=ALU.min)
        logs = sbuf("logs", [P, 4, N], F32)
        for q in range(4):
            nc.scalar.activation(out=logs[:, q, :], in_=capped[:, q, :], func=ACT.Ln, bias=1.0)

        nxt = [sbuf("nxt0", [P, PACK, QUARTER], F32)]
        if NEXT_ON_VECTOR == 2:
            nxt.append(sbuf("nxt1", [P, PACK, QUARTER], F32, tag="expo_tail"))
        late = sbuf("nxt_late", [P, 4 - NEXT_ON_VECTOR, PACK, QUARTER], F32, tag="capped")
        nxt = [t[:] for t in nxt] + [late[:, i] for i in range(4 - NEXT_ON_VECTOR)]
        for q in range(4):
            for j in range(PACK):
                window = clr[:, j, :].indirect(nxo_t[:, 8 * q : 8 * q + 8])
                if q < NEXT_ON_VECTOR:
                    nc.vector.tensor_copy(out=nxt[q][:, j, :], in_=window)
                else:
                    nc.scalar.activation(out=nxt[q][:, j, :], in_=window, func=ACT.Copy)

        out_rows = out_0.rearrange("(p j) e -> p j e", j=PACK)
        out_words = out_1[0].rearrange("p e r -> p (e r)").bitcast(I32)
        res_sc = sbuf("res_sc", [P, N], U8)
        res_bf = sbuf("res_bf", [P, N * PACK], BF16)
        pen, prod, res = {}, {}, {}

        def penalty(q):
            pen[q] = sbuf("pen%d" % q, [P, PACK, QUARTER], F32)
            nc.vector.scalar_tensor_tensor(
                out=pen[q][:], in0=clr[:, :, quarters[q]], scalar=-4.0, in1=by_rows(logs[:, q, :]), op0=ALU.mult, op1=ALU.max
            )

        def product(q):
            prod[q] = sbuf("prod%d" % q, [P, PACK, QUARTER], F32)
            nc.vector.tensor_tensor(out=prod[q][:], in0=sc[q][:], in1=pen[q][:], op=ALU.mult)

        def result(q):
            res[q] = sbuf("res%d" % q, [P, PACK, QUARTER], F32)
            nc.vector.scalar_tensor_tensor(
                out=res[q][:],
                in0=nxt[q],
                scalar=-0.6,
                in1=prod[q][:],
                op0=ALU.mult,
                op1=ALU.add,
            )
            nc.sync.dma_start(out=out_rows[:, :, quarters[q]], in_=res[q][:])

        def interleave(q, copy):
            copy(
                out=res_bf[:, q * N : (q + 1) * N].rearrange("p (c i j) -> p c j i", i=4, j=PACK),
                in_=res[q][:].rearrange("p j (c i) -> p c j i", i=4),
            )

        def planes(name, first, last, tag):
            cols = slice(first * QUARTER, last * QUARTER)
            codes = sbuf(name, [P, (last - first) * QUARTER], U32, tag=tag)
            nc.vector.quantize_mx(out=codes[:].bitcast(FP8X4), scales=res_sc[:, cols], in_=res_bf[:, first * N : last * N])
            nc.scalar.dma_start(out=out_words[:, cols], in_=codes[:].bitcast(I32))

        stages = (penalty, product, result)
        for step in range(4 + len(stages) - 1):
            for k in range(len(stages)):
                if 0 <= step - k < 4:
                    stages[k](step - k)
            if 2 <= step < 5:
                interleave(step - 2, nc.scalar.copy)
        planes("codes_head", 0, 3, "prod3")
        interleave(3, nc.vector.tensor_copy)
        planes("codes_tail", 3, 4, None)
        for q in range(4):
            queue = nc.sync if q % 2 else nc.scalar
            queue.dma_start(
                out=out_2[0, 4 * q : 4 * q + 4, :].bitcast(I32), in_=res_sc[32 * q : 32 * q + 4, :].bitcast(I32)
            )
